import numpy as np, ml_dtypes
CORES = [23,119,17,113]
N = 4
BF = ml_dtypes.bfloat16
S, R, B, CAP = 768, 256, 1, 320
L, IT, I = 1, 8, 8
D, TOP, F = 1, 1, 1
def where_to(rep):
    i = np.arange(N * S); first = np.maximum.accumulate(np.where(rep == 0, i, 0)); rec = np.add.accumulate((rep == 0).astype(np.int64)) - 1
    return rec, 0 * i, i - first
def count(rec):
    return np.bincount(np.arange(N * S) // S * N + rec // B % N, minlength=N * N)
def parts(rng, lens, total):
    diff = int(total - np.sum(lens)); room = I - lens if diff > 0 else lens - 1
    k = np.bincount(rng.permutation(np.repeat(np.arange(len(lens)), room))[:abs(diff)], minlength=len(lens))
    return lens + (k if diff > 0 else -k)
def rich(rng, n, total):
    return parts(rng, np.where(rng.random(n) * ((I - 1) * n) < 2 * (total - n), rng.integers(1, I + 1, n), 1), total)
def levels(rng, lens):
    if count(np.repeat(np.arange(len(lens)), lens)).max() > CAP:
        lens = np.diff(np.arange(N * R + 1) * (N * S) // (N * R))
    rep = np.full(N * S, TOP, np.int32); rep[np.add.accumulate(lens) - lens] = 0
    if L > 1:
        u = rng.random(N * S).tolist(); i = 0
        for n in lens.tolist():
            k = c = 1
            for j in range(1, n):
                if c == IT or (k < L and n - j <= (L - k) * IT and u[i + j] < 0.35):
                    rep[i + j] = 1; k += 1; c = 1
                else: c += 1
            i += n
    return rep
def values(rng):
    return rng.integers(0, 1 << 20, (N, 8, S)).astype(np.int32)
def make(rng, cols, p):
    rl = np.ascontiguousarray(np.stack([levels(rng, c) for c in cols]).reshape(8, N, S).transpose(1, 0, 2))
    dl = np.where(rng.random((N, 8, S)) < p, D, rng.integers(0, D, (N, 8, S))).astype(np.int32)
    return {"rl": rl, "dl": dl, "val": values(rng)}
def setup_inputs(rng):
    cols = [rich(rng, int(rng.integers(N * R * 3 // 4, N * R + 1)), N * S) for g in range(8)]
    return make(rng, cols, rng.integers(4, 16, (N, 8, 1)) * 0.0625)
def setup_inputs_full(rng):
    cols = []; mix = rng.permutation(8).tolist(); odd = mix[:4]; home = mix[4]; m = R // N
    for g in range(8):
        if g in odd: cols.append(rich(rng, N * R, N * S)); continue
        c = []
        for q in range(N):
            d = q if g == home else (q + 1 + g % (N - 1)) % N; own = np.arange(R) // B % N == d; v = np.ones(R, np.int64)
            v[own] = parts(rng, v[own], CAP); v[~own] = parts(rng, v[~own], S - CAP); c.append(v)
        cols.append(np.concatenate(c))
    return make(rng, cols, rng.choice(np.array([0.5, 1.0]), (N, 8, 1)))
def setup_inputs_edges(rng):
    cols = []
    for g in range(8):
        a = rng.integers(0, I + 1, N - 1); c = []; at = 0
        if g < 4: a[:] = (0, I, 1, I - 1)[g]
        for q in range(1, N + 1):
            end = q * S - int(a[q - 1]) if q < N else N * S; seg = end - at
            c.append(rich(rng, max(-(-seg // I), seg * R * int(rng.integers(12, 17)) // (16 * S)), seg))
            if q < N: c.append(np.array([I])); at = end + I
        cols.append(np.concatenate(c))
    return make(rng, cols, rng.integers(0, 3, (N, 8, 1)) * 0.5)
def setup_inputs_few(rng):
    cols = []
    for g in range(8):
        h = int(rng.integers(1, I + 1)) if g else I; k = (N * S - h) // I; t = N * S - h - k * I
        cols.append(np.array([h] + [I] * k + ([t] if t else [])))
    p = rng.integers(8, 17, (N, 8, 1)) * 0.0625; p[:, rng.integers(0, 8)] = 0
    return make(rng, cols, p)
def setup_inputs_spread(rng):
    cols = [rich(rng, int(rng.integers(N * S // I, N * R + 1)), N * S) for g in range(8)]
    d = make(rng, cols, rng.integers(1, 16, (N, 8, 1)) * 0.0625)
    v = d["val"] >> rng.integers(0, 21, (N, 8, S)); d["val"] = np.where(rng.random((N, 8, S)) < 0.0625, (1 << 20) - 1, v).astype(np.int32)
    return d
def check_inputs(d):
    rl, dl, val = d["rl"], d["dl"], d["val"]; bad = []
    if not (((rl >= 0) & (rl <= TOP)).all() and ((dl >= 0) & (dl <= D)).all()): bad.append("levels")
    if not (rl[0, :, 0] == 0).all(): bad.append("first")
    if not (((val >= 0) & (val < 1 << 20)).all()): bad.append("values")
    if bad: return bad
    for g in range(8):
        rec, lst, item = where_to(rl[:, g].reshape(-1))
        if rec[-1] >= N * R: bad.append("records")
        if lst.max() >= L or item.max() >= IT: bad.append("items")
        if count(rec).max() > CAP: bad.append("pairs")
    return sorted(set(bad))
def reference(rl, dl, val):
    y = np.full((N, 8, F, R * I), -2, np.float32); x = val.reshape(N, 8, F, S); q = np.arange(N * S) // S
    for g in range(8):
        rec, lst, item = where_to(rl[:, g].reshape(-1)); lev = dl[:, g].reshape(-1)
        has = (dl[:, g] == D).astype(np.int64); v = (np.add.accumulate(has, axis=1) - has).reshape(-1)
        e = np.where((lev == D)[:, None], x[q, g, :, v].astype(np.float32), (lev - D)[:, None])
        y[rec // B % N, g, :, (rec // (B * N) * B + rec % B) * I + lst * IT + item] = e
    return {"y": y.reshape(N, 8 * F, R * I).astype(np.float32)}

@@ -1,0 +1,280 @@
+from concourse.bass import DstId, RemoteDMATransfer
+from concourse.mybir import dt, AluOpType, AxisListType, ActivationFunctionType
+
+N = 4
+C = 48
+W = 8192
+SCRATCH = {
+    "rli": ("sbuf", [128, C], "int32"),
+    "dli": ("sbuf", [128, C], "int32"),
+    "vali": ("sbuf", [128, 776], "int32"),
+    "va": ("sbuf", [128, 776], "int32"),
+    "rlb": ("sbuf", [128, C], "bfloat16"),
+    "dlb": ("sbuf", [128, C], "bfloat16"),
+    "sc": ("sbuf", [128, 2 * C], "bfloat16"),
+    "dsc": ("sbuf", [128, C], "bfloat16"),
+    "vi": ("sbuf", [128, C], "float32"),
+    "vm": ("sbuf", [128, C], "float32"),
+    "vl": ("sbuf", [128, C], "uint16"),
+    "i1": ("sbuf", [128, C], "float32"),
+    "nn": ("sbuf", [128, C], "float32"),
+    "st": ("sbuf", [128, C], "float32"),
+    "rl4": ("sbuf", [128, C], "float32"),
+    "ns": ("sbuf", [128, C], "float32"),
+    "d1": ("sbuf", [128, C], "float32"),
+    "ll": ("sbuf", [128, C], "float32"),
+    "zl": ("sbuf", [128, C], "float32"),
+    "si": ("sbuf", [128, C], "int32"),
+    "tt": ("sbuf", [128, C], "float32"),
+    "oo": ("sbuf", [128, C], "float32"),
+    "ol": ("sbuf", [128, C], "uint16"),
+    "data": ("sbuf", [128, 768], "int32"),
+    "win": ("sbuf", [128, W], "bfloat16"),
+    "ones": ("sbuf", [128, 128], "bfloat16"),
+    "onesf": ("sbuf", [128, 128], "float32"),
+    "t1": ("sbuf", [128, 128], "bfloat16"),
+    "bd": ("sbuf", [128, 128], "bfloat16"),
+    "lt": ("sbuf", [128, 128], "bfloat16"),
+    "bdn": ("sbuf", [128, 128], "bfloat16"),
+    "ltn": ("sbuf", [128, 128], "bfloat16"),
+    "sh": ("sbuf", [128, 128], "bfloat16"),
+    "wr": ("sbuf", [128, 128], "bfloat16"),
+    "sh4": ("sbuf", [128, 128], "bfloat16"),
+    "wr4": ("sbuf", [128, 128], "bfloat16"),
+    "ident": ("sbuf", [128, 128], "float32"),
+    "z8": ("sbuf", [128, 8], "float32"),
+    "s8a": ("sbuf", [128, 8], "float32"),
+    "s8b": ("sbuf", [128, 8], "float32"),
+    "s8c": ("sbuf", [128, 8], "float32"),
+    "zb8": ("sbuf", [128, 8], "bfloat16"),
+    "w8a": ("sbuf", [128, 8], "bfloat16"),
+    "w8b": ("sbuf", [128, 8], "bfloat16"),
+    "w8c": ("sbuf", [128, 8], "bfloat16"),
+    "sl": ("sbuf", [128, 1], "float32"),
+    "bl": ("sbuf", [128, 1], "float32"),
+    "pi": ("sbuf", [128, 1], "int32"),
+    "pa": ("sbuf", [128, 1], "int32"),
+    "kl": ("sbuf", [128, 1], "float32"),
+    "kz": ("sbuf", [128, 1], "float32"),
+    "ysb": ("sbuf", [128, 128], "float32"),
+    "ps_d": ("psum", [128, 512], "float32"),
+    "ps_b": ("psum", [128, 512], "float32"),
+    "ps_c": ("psum", [128, 512], "float32"),
+    "ps_y": ("psum", [128, 512], "float32"),
+}
+for _q in range(N):
+    SCRATCH["cm%d" % _q] = ("sbuf", [128, 50], "bfloat16")
+    SCRATCH["rc%d" % _q] = ("sbuf", [128, 128], "float32")
+    SCRATCH["ob%d" % _q] = ("sbuf", [128, 128], "float32")
+    SCRATCH["ps_o%d" % _q] = ("psum", [128, 512], "float32")
+SEMAPHORES = ["srl", "sdl", "sval", "sy", "sv", "sg", "ss", "sp", "rcnt", "lr"] + ["rd%d" % q for q in range(N)]
+
+
+def first_engines(topo, cores, q):
+    off = [d for d in range(q + 1, N) if topo.chip(cores[d]) != topo.chip(cores[q])]
+    on = [d for d in range(q + 1, N) if topo.chip(cores[d]) == topo.chip(cores[q])]
+    res = {}
+    used = []
+    for i, d in enumerate(off):
+        e = topo.engines(cores[q], cores[d])
+        n = len(e) // 2
+        res[d] = e[i * n:(i + 1) * n]
+        used += e
+    for d in on:
+        res[d] = [x for x in topo.engines(cores[q], cores[d]) if x not in used]
+    return res
+
+
+def rank_program(g, core, T, topo):
+    rank = T.rank_of(core)
+    if rank is None:
+        return
+    cores = list(T.cores)
+    q = rank
+    S = T.sem
+    A = AluOpType
+    ACT = ActivationFunctionType
+    queues = {"v": g.vector, "s": g.scalar, "p": g.tensor, "g": g, "y": g.sync}
+    own = {"v": "sv", "s": "ss", "p": "sp", "g": "sg"}
+    done = {"v": 0, "s": 0, "p": 0, "g": 0}
+    seen = {}
+
+    def wait(qn, sem, val):
+        if val > seen.get((qn, sem), 0):
+            seen[(qn, sem)] = val
+            queues[qn].wait_ge(S[sem], val)
+
+    def after(qn, *marks):
+        for (o, c) in marks:
+            wait(qn, own[o], c)
+
+    def mark(qn, ins):
+        ins.then_inc(S[own[qn]], 1)
+        done[qn] += 1
+        return (qn, done[qn])
+
+    V = g.vector
+    g.sync.dma_start(T.rli[:], T.rl[:]).then_inc(S.srl, 16)
+    g.scalar.dma_start(T.dli[:], T.dl[:]).then_inc(S.sdl, 16)
+    m_ones = mark("v", V.memset(T.ones[:], 1.0))
+    m_z8 = mark("v", V.memset(T.z8[:], 0.0))
+    m_vm = mark("v", V.memset(T.vali[:], -1))
+    after("y", m_vm)
+    for k in range(3):
+        g.sync.dma_start(T.vali[k::16, 1:769], T.val[:]).then_inc(S.sval, 16)
+    m_f0 = mark("v", V.memset(T.win[:, 0:1024], 0.0))
+    m_onesf = mark("v", V.memset(T.onesf[:], 1.0))
+    m_zb8 = mark("v", V.memset(T.zb8[:], 0.0))
+
+    after("g", m_ones)
+    m_t1 = mark("g", g.affine_select(T.t1[:], T.ones[:], [[-16, 8], [0, 16]], A.is_ge, 0.0, 0, 1))
+    after("g", m_t1)
+    m_bd = mark("g", g.affine_select(T.bd[:], T.t1[:], [[16, 8], [0, 16]], A.is_ge, 0.0, 15, -1))
+    after("g", m_bd)
+    m_lt = mark("g", g.affine_select(T.lt[:], T.bd[:], [[1, 128]], A.is_gt, 0.0, 0, -1))
+    after("g", m_z8)
+    m = mark("g", g.affine_select(T.s8a[:], T.z8[:], [[-16, 8]], A.not_equal, 1.0, 0, 1))
+    after("g", m)
+    m = mark("g", g.affine_select(T.s8b[:], T.s8a[:], [[-16, 8]], A.not_equal, 2.0 ** -8, -1, 1))
+    after("g", m)
+    m_s8 = mark("g", g.affine_select(T.s8c[:], T.s8b[:], [[-16, 8]], A.not_equal, 2.0 ** -16, -2, 1))
+
+    after("s", m_f0)
+    m_fs = None
+    for k in range(1, 6):
+        m_fs = mark("s", g.scalar.activation(T.win[:, 1024 * k:1024 * k + 1024], T.win[:, 0:1024], ACT.Copy))
+
+    wait("v", "srl", 16)
+    m = mark("v", V.tensor_copy(T.rlb[:], T.rli[:]))
+    after("v", m)
+    m_c = mark("v", V.tensor_tensor_scan(T.sc[:, 0:C], T.ones[:, 0:C], T.rlb[:], 0.0, A.mult, A.add))
+    m_it = mark("v", V.tensor_tensor_scan(T.sc[:, C:2 * C], T.rlb[:], T.rlb[:], 0.0, A.mult, A.add))
+    fe = first_engines(topo, cores, q)
+    lr = 0
+    if fe:
+        after("g", m_it)
+        tr = []
+        for d in sorted(fe):
+            a = topo.addr(cores[d])
+            tr.append(RemoteDMATransfer(dst_ids=[DstId(rid=a[0], pnc=a[1])], dma_engine_mask=sum(1 << e for e in fe[d]),
+                                        remote_sem=S.rcnt, src=T.sc[:, C - 1:2 * C], dst=T["cm%d" % q][:, 0:C + 1]))
+            lr += len(fe[d])
+        g.remote_dma_fused(tr, local_sem=S.lr)
+
+    wait("v", "sdl", 16)
+    m_dlb = mark("v", V.tensor_copy(T.dlb[:], T.dli[:]))
+    after("v", m_dlb)
+    m_ds = mark("v", V.tensor_tensor_scan(T.dsc[:], T.ones[:, 0:C], T.dlb[:], 0.0, A.mult, A.add))
+    after("p", m_ds, m_lt)
+    m_pd = mark("p", g.tensor.matmul(T.ps_d[:, 0:1], T.lt[:], T.dsc[:, C - 1:C], True, True))
+    after("v", m_s8)
+    m = mark("v", V.tensor_reduce(T.sl[:], T.s8c[:], AxisListType.X, A.add))
+    after("v", m)
+    m_bl = mark("v", V.tensor_scalar(T.bl[:], T.sl[:], 2.5, -0.5, A.mult, A.add))
+    after("v", m_pd)
+    m = mark("v", V.tensor_tensor_scan(T.vi[:], T.ones[:, 0:C], T.dlb[:], T.ps_d[:, 0:1], A.mult, A.add))
+    after("v", m)
+    m = mark("v", V.tensor_tensor(T.vm[:], T.vi[:], T.dlb[:], A.mult))
+    after("v", m)
+    m_vl = mark("v", V.tensor_copy(T.vl[:], T.vm[:]))
+    wait("v", "sval", 48)
+    after("v", m_bl)
+    m = mark("v", V.tensor_scalar(T.va[:], T.vali[:], T.sl[:, 0:1], T.bl[:, 0:1], A.mult, A.add))
+    after("v", m, m_vl)
+    m_data = mark("v", V.tensor_scalar(T.data[:], T.va[:, 0:776].indirect(T.vl[:, 0:C]), 255, None, A.bitwise_and))
+
+    m_iota = mark("g", g.iota(T.pi[:], [[0, 1]], 0, 1))
+    m_i1 = mark("g", g.iota(T.i1[:], [[1, C]], 1, 0, allow_small_or_imprecise_dtypes=True))
+    m_sh = mark("g", g.affine_select(T.sh[:], T.bd[:], [[1, 128]], A.is_equal, 0.0, -1, -1))
+    m_wr = mark("g", g.affine_select(T.wr[:], T.ones[:], [[-16, 8], [-1000, 16]], A.is_equal, 0.0, -15, 1))
+    after("g", m_zb8)
+    m = mark("g", g.affine_select(T.w8a[:], T.zb8[:], [[-16, 8]], A.not_equal, 1.0, 0, 1))
+    after("g", m)
+    m = mark("g", g.affine_select(T.w8b[:], T.w8a[:], [[-16, 8]], A.not_equal, 256.0, -1, 1))
+    after("g", m)
+    m_w8 = mark("g", g.affine_select(T.w8c[:], T.w8b[:], [[-16, 8]], A.not_equal, 65536.0, -2, 1))
+    after("g", m_onesf)
+    m_id = mark("g", g.affine_select(T.ident[:], T.onesf[:], [[-1, 128]], A.is_equal, 0.0, 0, 1))
+
+    after("v", m_bd, m_lt)
+    m_bdn = mark("v", V.tensor_scalar(T.bdn[:], T.bd[:], -1.0, None, A.mult))
+    m_ltn = mark("v", V.tensor_scalar(T.ltn[:], T.lt[:], -1.0, None, A.mult))
+    m_st = mark("v", V.tensor_scalar(T.st[:], T.rlb[:], -1.0, 1.0, A.mult, A.add))
+    m_rl4 = mark("v", V.tensor_scalar(T.rl4[:], T.rlb[:], 4.0, None, A.mult))
+    after("v", m_iota, m_i1)
+    m_nn = mark("v", V.tensor_tensor(T.nn[:], T.i1[:], T.sc[:, 0:C], A.subtract))
+    m_pa = mark("v", V.tensor_scalar(T.pa[:], T.pi[:], 15, None, A.bitwise_and))
+    after("v", m_nn)
+    m_ns = mark("v", V.tensor_tensor(T.ns[:], T.nn[:], T.st[:], A.mult))
+    after("v", m_pa)
+    k0 = 1.0 * C * 16 * q
+    m_kl = mark("v", V.tensor_scalar(T.kl[:], T.pa[:], 1.0 * C, k0 - 2.5, A.mult, A.add))
+    m_kz = mark("v", V.tensor_scalar(T.kz[:], T.pa[:], 1.0 * C, k0 - 1.0, A.mult, A.add))
+    after("v", m_ns)
+    m_d1 = mark("v", V.tensor_tensor(T.d1[:], T.ns[:], T.rl4[:], A.add))
+    after("v", m_kl)
+    m_ll = mark("v", V.tensor_scalar(T.ll[:], T.nn[:], T.kl[:, 0:1], None, A.add))
+    after("v", m_sh, m_wr)
+    m_sh4 = mark("v", V.tensor_scalar(T.sh4[:], T.sh[:], 4.0, None, A.mult))
+    m_wr4 = mark("v", V.tensor_scalar(T.wr4[:], T.wr[:], 4.0, None, A.mult))
+    m_fv = mark("v", V.memset(T.win[:, 6144:W], 0.0))
+
+    after("p", m_sh4, m_it)
+    m_pc = mark("p", g.tensor.matmul(T.ps_c[:, 0:1], T.sh4[:], T.sc[:, 2 * C - 1:2 * C], True, q == 0))
+    after("p", m_ltn)
+    m_pb = mark("p", g.tensor.matmul(T.ps_b[:, 0:1], T.ltn[:], T.sc[:, C - 1:C], True, q == 0))
+    if q:
+        after("p", m_wr4, m_bdn)
+        tot = sum(len(first_engines(topo, cores, j)[q]) for j in range(q))
+        wait("p", "rcnt", tot)
+        m_pc = mark("p", g.tensor.matmul(T.ps_c[:, 0:1], T.wr4[:], T["cm%d" % (q - 1)][:, C:C + 1], False, True))
+        for j in range(q):
+            m_pb = mark("p", g.tensor.matmul(T.ps_b[:, 0:1], T.bdn[:], T["cm%d" % j][:, 0:1], False, j == q - 1))
+    after("v", m_pc, m_d1)
+    m_zl = mark("v", V.tensor_tensor_scan(T.zl[:], T.rlb[:], T.d1[:], T.ps_c[:, 0:1], A.mult, A.add))
+    after("v", m_pb, m_ll)
+    m = mark("v", V.tensor_scalar(T.si[:], T.ll[:], T.ps_b[:, 0:1], 0.25, A.add, A.mult))
+    after("v", m)
+    m = mark("v", V.tensor_scalar(T.tt[:], T.si[:], 28.0, T.ps_b[:, 0:1], A.mult, A.add))
+    after("v", m, m_zl)
+    m = mark("v", V.tensor_tensor(T.oo[:], T.tt[:], T.zl[:], A.add))
+    after("v", m, m_kz)
+    m_ol = mark("v", V.tensor_scalar(T.ol[:], T.oo[:], T.kz[:, 0:1], None, A.add))
+    after("v", m_ol, m_data, m_fv, m_fs)
+    m_sct = mark("v", V.tensor_copy(T.win[:, 0:W].indirect(T.ol[:, 0:C]), T.data[:]))
+
+    others = [(q + 1) % N, (q + 3) % N, (q + 2) % N]
+    dests = [d for d in others if topo.chip(cores[d]) != topo.chip(core)]
+    dests += [d for d in others if d not in dests]
+    after("p", m_sct, m_w8)
+    mp = {}
+    for d in dests + [q]:
+        for b in range(16):
+            ins = g.tensor.matmul(T["ps_o%d" % d][:, b:128:16], T.win[:, 512 * b + d:512 * b + 512:4], T.w8c[:], True, True)
+        mp[d] = mark("p", ins)
+    mo = {}
+    for d in dests + [q]:
+        after("s", mp[d])
+        mo[d] = mark("s", g.scalar.activation(T["ob%d" % d][:], T["ps_o%d" % d][:, 0:128], ACT.Copy))
+        if d != q:
+            after("g", mo[d])
+            a = topo.addr(cores[d])
+            g.remote_dma(out_ap=T["rc%d" % q][:], in_ap=T["ob%d" % d][:], remote_sem=S["rd%d" % q], local_sem=S.lr,
+                         pid=a[1], routing_id=a[0], dma_engine_mask=topo.mask(core, cores[d]))
+            lr += len(topo.engines(core, cores[d]))
+
+    after("p", mo[q], m_id)
+    mark("p", g.tensor.matmul(T.ps_y[:, 0:128], T["ob%d" % q][:], T.ident[:], True, False))
+    src = [(q + 3) % N, (q + 2) % N, (q + 1) % N]
+    for i, j in enumerate(src):
+        wait("p", "rd%d" % j, len(topo.engines(cores[j], core)))
+        m_y = mark("p", g.tensor.matmul(T.ps_y[:, 0:128], T["rc%d" % j][:], T.ident[:], False, i == len(src) - 1))
+    after("v", m_y)
+    m_ys = mark("v", V.tensor_scalar(T.ysb[:], T.ps_y[:, 0:128], -2.0, None, A.add))
+    after("y", m_ys)
+    g.sync.dma_start(T.y[:], T.ysb[:]).then_inc(S.sy, 16)
+    g.sync.wait_ge(S.sy, 16)
+    for qn in ("v", "s", "p", "g"):
+        if done[qn]:
+            wait("g", own[qn], done[qn])
+    wait("g", "lr", lr)

@@ -3,7 +3,8 @@ from concourse.mybir import dt, AluOpType, AxisListType, ActivationFunctionType
 
 N = 4
 C = 48
-W = 8192
+BL = 12
+W = 512 * BL
 SCRATCH = {
     "rli": ("sbuf", [128, C], "int32"),
     "dli": ("sbuf", [128, C], "int32"),
@@ -30,17 +31,16 @@ SCRATCH = {
     "ol": ("sbuf", [128, C], "uint16"),
     "data": ("sbuf", [128, 768], "int32"),
     "win": ("sbuf", [128, W], "bfloat16"),
-    "ones": ("sbuf", [128, 128], "bfloat16"),
+    "neg": ("sbuf", [128, 128], "bfloat16"),
+    "four": ("sbuf", [128, 128], "bfloat16"),
+    "ones": ("sbuf", [128, C], "bfloat16"),
     "onesf": ("sbuf", [128, 128], "float32"),
     "t1": ("sbuf", [128, 128], "bfloat16"),
     "bd": ("sbuf", [128, 128], "bfloat16"),
     "lt": ("sbuf", [128, 128], "bfloat16"),
-    "bdn": ("sbuf", [128, 128], "bfloat16"),
-    "ltn": ("sbuf", [128, 128], "bfloat16"),
+    "sh0": ("sbuf", [128, 128], "bfloat16"),
     "sh": ("sbuf", [128, 128], "bfloat16"),
     "wr": ("sbuf", [128, 128], "bfloat16"),
-    "sh4": ("sbuf", [128, 128], "bfloat16"),
-    "wr4": ("sbuf", [128, 128], "bfloat16"),
     "ident": ("sbuf", [128, 128], "float32"),
     "z8": ("sbuf", [128, 8], "float32"),
     "s8a": ("sbuf", [128, 8], "float32"),
@@ -114,24 +114,27 @@ def rank_program(g, core, T, topo):
         return (qn, done[qn])
 
     V = g.vector
+    b0 = 24 * q // 16
     g.sync.dma_start(T.rli[:], T.rl[:]).then_inc(S.srl, 16)
     g.scalar.dma_start(T.dli[:], T.dl[:]).then_inc(S.sdl, 16)
-    m_ones = mark("v", V.memset(T.ones[:], 1.0))
+    m_neg = mark("v", V.memset(T.neg[:], -1.0))
     m_z8 = mark("v", V.memset(T.z8[:], 0.0))
+    m_f0 = mark("v", V.memset(T.win[:, 0:1024], 0.0))
     m_vm = mark("v", V.memset(T.vali[:], -1))
     after("y", m_vm)
     for k in range(3):
         g.sync.dma_start(T.vali[k::16, 1:769], T.val[:]).then_inc(S.sval, 16)
-    m_f0 = mark("v", V.memset(T.win[:, 0:1024], 0.0))
+    m_ones = mark("v", V.memset(T.ones[:], 1.0))
+    m_four = mark("v", V.memset(T.four[:], 4.0))
     m_onesf = mark("v", V.memset(T.onesf[:], 1.0))
     m_zb8 = mark("v", V.memset(T.zb8[:], 0.0))
+    for d in range(N):
+        m_po = mark("v", V.memset(T["ps_o%d" % d][:, 0:128], 0.0))
 
-    after("g", m_ones)
-    m_t1 = mark("g", g.affine_select(T.t1[:], T.ones[:], [[-16, 8], [0, 16]], A.is_ge, 0.0, 0, 1))
+    after("g", m_neg)
+    m_t1 = mark("g", g.affine_select(T.t1[:], T.neg[:], [[-16, 8], [0, 16]], A.is_ge, 0.0, 0, 1))
     after("g", m_t1)
-    m_bd = mark("g", g.affine_select(T.bd[:], T.t1[:], [[16, 8], [0, 16]], A.is_ge, 0.0, 15, -1))
-    after("g", m_bd)
-    m_lt = mark("g", g.affine_select(T.lt[:], T.bd[:], [[1, 128]], A.is_gt, 0.0, 0, -1))
+    m_lt = mark("g", g.affine_select(T.lt[:], T.t1[:], [[1, 128]], A.is_gt, 0.0, 0, -1))
     after("g", m_z8)
     m = mark("g", g.affine_select(T.s8a[:], T.z8[:], [[-16, 8]], A.not_equal, 1.0, 0, 1))
     after("g", m)
@@ -140,14 +143,14 @@ def rank_program(g, core, T, topo):
     m_s8 = mark("g", g.affine_select(T.s8c[:], T.s8b[:], [[-16, 8]], A.not_equal, 2.0 ** -16, -2, 1))
 
     after("s", m_f0)
-    m_fs = None
-    for k in range(1, 6):
+    for k in range(1, 5):
         m_fs = mark("s", g.scalar.activation(T.win[:, 1024 * k:1024 * k + 1024], T.win[:, 0:1024], ACT.Copy))
+    m_fs = mark("s", g.scalar.activation(T.win[:, 5120:5632], T.win[:, 0:512], ACT.Copy))
 
     wait("v", "srl", 16)
     m = mark("v", V.tensor_copy(T.rlb[:], T.rli[:]))
     after("v", m)
-    m_c = mark("v", V.tensor_tensor_scan(T.sc[:, 0:C], T.ones[:, 0:C], T.rlb[:], 0.0, A.mult, A.add))
+    m_c = mark("v", V.tensor_tensor_scan(T.sc[:, 0:C], T.ones[:], T.rlb[:], 0.0, A.mult, A.add))
     m_it = mark("v", V.tensor_tensor_scan(T.sc[:, C:2 * C], T.rlb[:], T.rlb[:], 0.0, A.mult, A.add))
     fe = first_engines(topo, cores, q)
     lr = 0
@@ -164,7 +167,7 @@ def rank_program(g, core, T, topo):
     wait("v", "sdl", 16)
     m_dlb = mark("v", V.tensor_copy(T.dlb[:], T.dli[:]))
     after("v", m_dlb)
-    m_ds = mark("v", V.tensor_tensor_scan(T.dsc[:], T.ones[:, 0:C], T.dlb[:], 0.0, A.mult, A.add))
+    m_ds = mark("v", V.tensor_tensor_scan(T.dsc[:], T.ones[:], T.dlb[:], 0.0, A.mult, A.add))
     after("p", m_ds, m_lt)
     m_pd = mark("p", g.tensor.matmul(T.ps_d[:, 0:1], T.lt[:], T.dsc[:, C - 1:C], True, True))
     after("v", m_s8)
@@ -172,11 +175,11 @@ def rank_program(g, core, T, topo):
     after("v", m)
     m_bl = mark("v", V.tensor_scalar(T.bl[:], T.sl[:], 2.5, -0.5, A.mult, A.add))
     after("v", m_pd)
-    m = mark("v", V.tensor_tensor_scan(T.vi[:], T.ones[:, 0:C], T.dlb[:], T.ps_d[:, 0:1], A.mult, A.add))
+    m = mark("v", V.tensor_tensor_scan(T.vi[:], T.ones[:], T.dlb[:], T.ps_d[:, 0:1], A.mult, A.subtract))
     after("v", m)
     m = mark("v", V.tensor_tensor(T.vm[:], T.vi[:], T.dlb[:], A.mult))
     after("v", m)
-    m_vl = mark("v", V.tensor_copy(T.vl[:], T.vm[:]))
+    m_vl = mark("v", V.tensor_scalar(T.vl[:], T.vm[:], -1.0, None, A.mult))
     wait("v", "sval", 48)
     after("v", m_bl)
     m = mark("v", V.tensor_scalar(T.va[:], T.vali[:], T.sl[:, 0:1], T.bl[:, 0:1], A.mult, A.add))
@@ -185,8 +188,12 @@ def rank_program(g, core, T, topo):
 
     m_iota = mark("g", g.iota(T.pi[:], [[0, 1]], 0, 1))
     m_i1 = mark("g", g.iota(T.i1[:], [[1, C]], 1, 0, allow_small_or_imprecise_dtypes=True))
-    m_sh = mark("g", g.affine_select(T.sh[:], T.bd[:], [[1, 128]], A.is_equal, 0.0, -1, -1))
-    m_wr = mark("g", g.affine_select(T.wr[:], T.ones[:], [[-16, 8], [-1000, 16]], A.is_equal, 0.0, -15, 1))
+    after("g", m_four)
+    m = mark("g", g.affine_select(T.sh0[:], T.four[:], [[1, 128]], A.is_equal, 0.0, -1, -1))
+    after("g", m)
+    m_sh = mark("g", g.affine_select(T.sh[:], T.sh0[:], [[0, 8], [1, 16]], A.is_gt, 0.0, 0, 0))
+    m_bd = mark("g", g.affine_select(T.bd[:], T.t1[:], [[16, 8], [0, 16]], A.is_ge, 0.0, 15, -1))
+    m_wr = mark("g", g.affine_select(T.wr[:], T.four[:], [[-16, 8], [-1000, 16]], A.is_equal, 0.0, -15, 1))
     after("g", m_zb8)
     m = mark("g", g.affine_select(T.w8a[:], T.zb8[:], [[-16, 8]], A.not_equal, 1.0, 0, 1))
     after("g", m)
@@ -196,9 +203,6 @@ def rank_program(g, core, T, topo):
     after("g", m_onesf)
     m_id = mark("g", g.affine_select(T.ident[:], T.onesf[:], [[-1, 128]], A.is_equal, 0.0, 0, 1))
 
-    after("v", m_bd, m_lt)
-    m_bdn = mark("v", V.tensor_scalar(T.bdn[:], T.bd[:], -1.0, None, A.mult))
-    m_ltn = mark("v", V.tensor_scalar(T.ltn[:], T.lt[:], -1.0, None, A.mult))
     m_st = mark("v", V.tensor_scalar(T.st[:], T.rlb[:], -1.0, 1.0, A.mult, A.add))
     m_rl4 = mark("v", V.tensor_scalar(T.rl4[:], T.rlb[:], 4.0, None, A.mult))
     after("v", m_iota, m_i1)
@@ -209,27 +213,23 @@ def rank_program(g, core, T, topo):
     after("v", m_pa)
     k0 = 1.0 * C * 16 * q
     m_kl = mark("v", V.tensor_scalar(T.kl[:], T.pa[:], 1.0 * C, k0 - 2.5, A.mult, A.add))
-    m_kz = mark("v", V.tensor_scalar(T.kz[:], T.pa[:], 1.0 * C, k0 - 1.0, A.mult, A.add))
+    m_kz = mark("v", V.tensor_scalar(T.kz[:], T.pa[:], 1.0 * C, k0 - 1.0 - 512.0 * b0, A.mult, A.add))
     after("v", m_ns)
     m_d1 = mark("v", V.tensor_tensor(T.d1[:], T.ns[:], T.rl4[:], A.add))
     after("v", m_kl)
     m_ll = mark("v", V.tensor_scalar(T.ll[:], T.nn[:], T.kl[:, 0:1], None, A.add))
-    after("v", m_sh, m_wr)
-    m_sh4 = mark("v", V.tensor_scalar(T.sh4[:], T.sh[:], 4.0, None, A.mult))
-    m_wr4 = mark("v", V.tensor_scalar(T.wr4[:], T.wr[:], 4.0, None, A.mult))
-    m_fv = mark("v", V.memset(T.win[:, 6144:W], 0.0))
+    m_fv = mark("v", V.memset(T.win[:, 5632:W], 0.0))
 
-    after("p", m_sh4, m_it)
-    m_pc = mark("p", g.tensor.matmul(T.ps_c[:, 0:1], T.sh4[:], T.sc[:, 2 * C - 1:2 * C], True, q == 0))
-    after("p", m_ltn)
-    m_pb = mark("p", g.tensor.matmul(T.ps_b[:, 0:1], T.ltn[:], T.sc[:, C - 1:C], True, q == 0))
+    after("p", m_sh, m_it)
+    m_pc = mark("p", g.tensor.matmul(T.ps_c[:, 0:1], T.sh[:], T.sc[:, 2 * C - 1:2 * C], True, q == 0))
+    m_pb = mark("p", g.tensor.matmul(T.ps_b[:, 0:1], T.lt[:], T.sc[:, C - 1:C], True, q == 0))
     if q:
-        after("p", m_wr4, m_bdn)
+        after("p", m_wr, m_bd)
         tot = sum(len(first_engines(topo, cores, j)[q]) for j in range(q))
         wait("p", "rcnt", tot)
-        m_pc = mark("p", g.tensor.matmul(T.ps_c[:, 0:1], T.wr4[:], T["cm%d" % (q - 1)][:, C:C + 1], False, True))
+        m_pc = mark("p", g.tensor.matmul(T.ps_c[:, 0:1], T.wr[:], T["cm%d" % (q - 1)][:, C:C + 1], False, True))
         for j in range(q):
-            m_pb = mark("p", g.tensor.matmul(T.ps_b[:, 0:1], T.bdn[:], T["cm%d" % j][:, 0:1], False, j == q - 1))
+            m_pb = mark("p", g.tensor.matmul(T.ps_b[:, 0:1], T.bd[:], T["cm%d" % j][:, 0:1], False, j == q - 1))
     after("v", m_pc, m_d1)
     m_zl = mark("v", V.tensor_tensor_scan(T.zl[:], T.rlb[:], T.d1[:], T.ps_c[:, 0:1], A.mult, A.add))
     after("v", m_pb, m_ll)
@@ -246,11 +246,11 @@ def rank_program(g, core, T, topo):
     others = [(q + 1) % N, (q + 3) % N, (q + 2) % N]
     dests = [d for d in others if topo.chip(cores[d]) != topo.chip(core)]
     dests += [d for d in others if d not in dests]
-    after("p", m_sct, m_w8)
+    after("p", m_sct, m_w8, m_po)
     mp = {}
     for d in dests + [q]:
-        for b in range(16):
-            ins = g.tensor.matmul(T["ps_o%d" % d][:, b:128:16], T.win[:, 512 * b + d:512 * b + 512:4], T.w8c[:], True, True)
+        for b in range(BL):
+            ins = g.tensor.matmul(T["ps_o%d" % d][:, b0 + b:128:16], T.win[:, 512 * b + d:512 * b + 512:4], T.w8c[:], True, True)
         mp[d] = mark("p", ins)
     mo = {}
     for d in dests + [q]:

@@ -4,58 +4,42 @@ from concourse.mybir import dt, AluOpType, AxisListType, ActivationFunctionType
 N = 4
 C = 48
 BL = 12
-W = 512 * BL
+W = 8208
 SCRATCH = {
     "rli": ("sbuf", [128, C], "int32"),
     "dli": ("sbuf", [128, C], "int32"),
-    "vali": ("sbuf", [128, 776], "int32"),
-    "va": ("sbuf", [128, 776], "int32"),
+    "vali": ("sbuf", [128, C], "int32"),
     "rlb": ("sbuf", [128, C], "bfloat16"),
     "dlb": ("sbuf", [128, C], "bfloat16"),
-    "sc": ("sbuf", [128, 2 * C], "bfloat16"),
+    "sc": ("sbuf", [128, 64], "bfloat16"),
     "dsc": ("sbuf", [128, C], "bfloat16"),
-    "vi": ("sbuf", [128, C], "float32"),
-    "vm": ("sbuf", [128, C], "float32"),
+    "nulk": ("sbuf", [128, C], "float32"),
+    "dm": ("sbuf", [128, C], "float32"),
     "vl": ("sbuf", [128, C], "uint16"),
-    "i1": ("sbuf", [128, C], "float32"),
-    "nn": ("sbuf", [128, C], "float32"),
-    "st": ("sbuf", [128, C], "float32"),
-    "rl4": ("sbuf", [128, C], "float32"),
-    "ns": ("sbuf", [128, C], "float32"),
-    "d1": ("sbuf", [128, C], "float32"),
+    "c0": ("sbuf", [128, C], "bfloat16"),
+    "c1": ("sbuf", [128, C], "bfloat16"),
+    "c2": ("sbuf", [128, C], "bfloat16"),
+    "rr": ("sbuf", [128, C], "float32"),
+    "rlk": ("sbuf", [128, C], "bfloat16"),
+    "bb": ("sbuf", [128, C], "bfloat16"),
     "ll": ("sbuf", [128, C], "float32"),
     "zl": ("sbuf", [128, C], "float32"),
     "si": ("sbuf", [128, C], "int32"),
     "tt": ("sbuf", [128, C], "float32"),
-    "oo": ("sbuf", [128, C], "float32"),
     "ol": ("sbuf", [128, C], "uint16"),
-    "data": ("sbuf", [128, 768], "int32"),
+    "vb": ("sbuf", [128, 776], "bfloat16"),
+    "data": ("sbuf", [128, 768], "bfloat16"),
     "win": ("sbuf", [128, W], "bfloat16"),
-    "neg": ("sbuf", [128, 128], "bfloat16"),
-    "four": ("sbuf", [128, 128], "bfloat16"),
-    "ones": ("sbuf", [128, C], "bfloat16"),
+    "ones": ("sbuf", [128, 128], "bfloat16"),
+    "four": ("sbuf", [128, C], "bfloat16"),
+    "zz": ("sbuf", [128, 144], "bfloat16"),
     "onesf": ("sbuf", [128, 128], "float32"),
     "t1": ("sbuf", [128, 128], "bfloat16"),
     "bd": ("sbuf", [128, 128], "bfloat16"),
     "lt": ("sbuf", [128, 128], "bfloat16"),
-    "sh0": ("sbuf", [128, 128], "bfloat16"),
-    "sh": ("sbuf", [128, 128], "bfloat16"),
+    "sh": ("sbuf", [128, 144], "bfloat16"),
     "wr": ("sbuf", [128, 128], "bfloat16"),
     "ident": ("sbuf", [128, 128], "float32"),
-    "z8": ("sbuf", [128, 8], "float32"),
-    "s8a": ("sbuf", [128, 8], "float32"),
-    "s8b": ("sbuf", [128, 8], "float32"),
-    "s8c": ("sbuf", [128, 8], "float32"),
-    "zb8": ("sbuf", [128, 8], "bfloat16"),
-    "w8a": ("sbuf", [128, 8], "bfloat16"),
-    "w8b": ("sbuf", [128, 8], "bfloat16"),
-    "w8c": ("sbuf", [128, 8], "bfloat16"),
-    "sl": ("sbuf", [128, 1], "float32"),
-    "bl": ("sbuf", [128, 1], "float32"),
-    "pi": ("sbuf", [128, 1], "int32"),
-    "pa": ("sbuf", [128, 1], "int32"),
-    "kl": ("sbuf", [128, 1], "float32"),
-    "kz": ("sbuf", [128, 1], "float32"),
     "ysb": ("sbuf", [128, 128], "float32"),
     "ps_d": ("psum", [128, 512], "float32"),
     "ps_b": ("psum", [128, 512], "float32"),
@@ -63,26 +47,42 @@ SCRATCH = {
     "ps_y": ("psum", [128, 512], "float32"),
 }
 for _q in range(N):
-    SCRATCH["cm%d" % _q] = ("sbuf", [128, 50], "bfloat16")
+    SCRATCH["cm%d" % _q] = ("sbuf", [128, 16], "bfloat16")
     SCRATCH["rc%d" % _q] = ("sbuf", [128, 128], "float32")
     SCRATCH["ob%d" % _q] = ("sbuf", [128, 128], "float32")
     SCRATCH["ps_o%d" % _q] = ("psum", [128, 512], "float32")
-SEMAPHORES = ["srl", "sdl", "sval", "sy", "sv", "sg", "ss", "sp", "rcnt", "lr"] + ["rd%d" % q for q in range(N)]
+SEMAPHORES = ["srl", "sdl", "sval", "slan", "sy", "sv", "sg", "ss", "sp", "rcnt", "lr"] + ["rd%d" % q for q in range(N)]
+
+
+def off_chip(topo, cores, q):
+    return [d for d in range(N) if topo.chip(cores[d]) != topo.chip(cores[q])]
 
 
 def first_engines(topo, cores, q):
-    off = [d for d in range(q + 1, N) if topo.chip(cores[d]) != topo.chip(cores[q])]
-    on = [d for d in range(q + 1, N) if topo.chip(cores[d]) == topo.chip(cores[q])]
     res = {}
     used = []
-    for i, d in enumerate(off):
+    for i, d in enumerate(x for x in off_chip(topo, cores, q) if x > q):
         e = topo.engines(cores[q], cores[d])
         n = len(e) // 2
         res[d] = e[i * n:(i + 1) * n]
         used += e
-    for d in on:
-        res[d] = [x for x in topo.engines(cores[q], cores[d]) if x not in used]
+    for d in range(q + 1, N):
+        if d not in res:
+            e = [x for x in topo.engines(cores[q], cores[d]) if x not in used]
+            res[d] = e[:4]
     return res
+
+
+def data_engines(topo, cores, q, d):
+    e = topo.engines(cores[q], cores[d])
+    off = off_chip(topo, cores, q)
+    if d not in off:
+        e = [x for x in e if x not in topo.engines(cores[q], cores[off[0]])]
+    return e
+
+
+def bits(e):
+    return sum(1 << x for x in e)
 
 
 def rank_program(g, core, T, topo):
@@ -115,43 +115,39 @@ def rank_program(g, core, T, topo):
 
     V = g.vector
     b0 = 24 * q // 16
+    w0 = 512 * b0
+    w1 = w0 + 512 * BL + 16
     g.sync.dma_start(T.rli[:], T.rl[:]).then_inc(S.srl, 16)
     g.scalar.dma_start(T.dli[:], T.dl[:]).then_inc(S.sdl, 16)
-    m_neg = mark("v", V.memset(T.neg[:], -1.0))
-    m_z8 = mark("v", V.memset(T.z8[:], 0.0))
-    m_f0 = mark("v", V.memset(T.win[:, 0:1024], 0.0))
-    m_vm = mark("v", V.memset(T.vali[:], -1))
-    after("y", m_vm)
-    for k in range(3):
-        g.sync.dma_start(T.vali[k::16, 1:769], T.val[:]).then_inc(S.sval, 16)
+    g.sync.dma_start(T.vali[:], T.val[:]).then_inc(S.sval, 16)
     m_ones = mark("v", V.memset(T.ones[:], 1.0))
+    m_f0 = mark("v", V.memset(T.win[:, w0:w0 + 512], -0.125))
     m_four = mark("v", V.memset(T.four[:], 4.0))
-    m_onesf = mark("v", V.memset(T.onesf[:], 1.0))
-    m_zb8 = mark("v", V.memset(T.zb8[:], 0.0))
-    for d in range(N):
-        m_po = mark("v", V.memset(T["ps_o%d" % d][:, 0:128], 0.0))
+    m_zz = mark("v", V.memset(T.zz[:], 0.0))
+    m_vb0 = mark("v", V.memset(T.vb[:, 0:8], -0.0625))
+    m_vb = mark("v", V.memset(T.vb[:, 8:776], 0.0))
 
-    after("g", m_neg)
-    m_t1 = mark("g", g.affine_select(T.t1[:], T.neg[:], [[-16, 8], [0, 16]], A.is_ge, 0.0, 0, 1))
+    after("g", m_ones)
+    m_t1 = mark("g", g.affine_select(T.t1[:], T.ones[:], [[-16, 8], [0, 16]], A.is_ge, 0.0, 0, 1))
     after("g", m_t1)
     m_lt = mark("g", g.affine_select(T.lt[:], T.t1[:], [[1, 128]], A.is_gt, 0.0, 0, -1))
-    after("g", m_z8)
-    m = mark("g", g.affine_select(T.s8a[:], T.z8[:], [[-16, 8]], A.not_equal, 1.0, 0, 1))
-    after("g", m)
-    m = mark("g", g.affine_select(T.s8b[:], T.s8a[:], [[-16, 8]], A.not_equal, 2.0 ** -8, -1, 1))
-    after("g", m)
-    m_s8 = mark("g", g.affine_select(T.s8c[:], T.s8b[:], [[-16, 8]], A.not_equal, 2.0 ** -16, -2, 1))
+
+    after("p", m_f0)
+    for d in range(N):
+        m_po = mark("p", g.tensor.matmul(T["ps_o%d" % d][:, 0:128], T.ones[0:16, 0:128], T.win[0:16, w0:w0 + 128], True, True))
 
     after("s", m_f0)
-    for k in range(1, 5):
-        m_fs = mark("s", g.scalar.activation(T.win[:, 1024 * k:1024 * k + 1024], T.win[:, 0:1024], ACT.Copy))
-    m_fs = mark("s", g.scalar.activation(T.win[:, 5120:5632], T.win[:, 0:512], ACT.Copy))
+    m = mark("s", g.scalar.activation(T.win[:, w0 + 512:w0 + 1024], T.win[:, w0:w0 + 512], ACT.Copy))
+    after("s", m)
+    for k in range(1, 3):
+        m_fs = mark("s", g.scalar.activation(T.win[:, w0 + 1024 * k:w0 + 1024 * k + 1024], T.win[:, w0:w0 + 1024], ACT.Copy))
+    w2 = w0 + 3072
 
     wait("v", "srl", 16)
-    m = mark("v", V.tensor_copy(T.rlb[:], T.rli[:]))
-    after("v", m)
-    m_c = mark("v", V.tensor_tensor_scan(T.sc[:, 0:C], T.ones[:], T.rlb[:], 0.0, A.mult, A.add))
-    m_it = mark("v", V.tensor_tensor_scan(T.sc[:, C:2 * C], T.rlb[:], T.rlb[:], 0.0, A.mult, A.add))
+    m_rlb = mark("v", V.tensor_copy(T.rlb[:], T.rli[:]))
+    after("v", m_rlb)
+    m_nn = mark("v", V.tensor_tensor_scan(T.sc[:, 0:C], T.ones[:, 0:C], T.rlb[:], 0.0, A.add, A.subtract))
+    m_it = mark("v", V.tensor_tensor_scan(T.sc[:, C:C + 8], T.rlb[:, C - 8:C], T.rlb[:, C - 8:C], 0.0, A.mult, A.add))
     fe = first_engines(topo, cores, q)
     lr = 0
     if fe:
@@ -159,118 +155,112 @@ def rank_program(g, core, T, topo):
         tr = []
         for d in sorted(fe):
             a = topo.addr(cores[d])
-            tr.append(RemoteDMATransfer(dst_ids=[DstId(rid=a[0], pnc=a[1])], dma_engine_mask=sum(1 << e for e in fe[d]),
-                                        remote_sem=S.rcnt, src=T.sc[:, C - 1:2 * C], dst=T["cm%d" % q][:, 0:C + 1]))
+            tr.append(RemoteDMATransfer(dst_ids=[DstId(rid=a[0], pnc=a[1])], dma_engine_mask=bits(fe[d]),
+                                        remote_sem=S.rcnt, src=T.sc[:, C - 1:C + 8], dst=T["cm%d" % q][:, 0:9]))
             lr += len(fe[d])
         g.remote_dma_fused(tr, local_sem=S.lr)
 
     wait("v", "sdl", 16)
     m_dlb = mark("v", V.tensor_copy(T.dlb[:], T.dli[:]))
+    wait("v", "sval", 16)
+    m_c0 = mark("v", V.tensor_copy(T.c0[:], T.vali[:]))
     after("v", m_dlb)
-    m_ds = mark("v", V.tensor_tensor_scan(T.dsc[:], T.ones[:], T.dlb[:], 0.0, A.mult, A.add))
+    m_ds = mark("v", V.tensor_tensor_scan(T.dsc[:], T.ones[:, 0:C], T.dlb[:], 0.0, A.mult, A.add))
+    after("v", m_c0)
+    m_rr = mark("v", V.tensor_tensor(T.rr[:], T.vali[:], T.c0[:], A.subtract))
+    m_nk = mark("v", V.tensor_scalar(T.nulk[:], T.dlb[:], 4096.0, -4089.0, A.mult, A.add))
+    after("v", m_rr)
+    m_c1 = mark("v", V.tensor_copy(T.c1[:], T.rr[:]))
+    after("v", m_nk)
+    m_dm = mark("v", V.tensor_tensor(T.dm[:], T.dsc[:], T.nulk[:], A.add))
+    after("v", m_c1)
+    m_c2 = mark("v", V.tensor_tensor(T.c2[:], T.rr[:], T.c1[:], A.subtract))
     after("p", m_ds, m_lt)
     m_pd = mark("p", g.tensor.matmul(T.ps_d[:, 0:1], T.lt[:], T.dsc[:, C - 1:C], True, True))
-    after("v", m_s8)
-    m = mark("v", V.tensor_reduce(T.sl[:], T.s8c[:], AxisListType.X, A.add))
-    after("v", m)
-    m_bl = mark("v", V.tensor_scalar(T.bl[:], T.sl[:], 2.5, -0.5, A.mult, A.add))
-    after("v", m_pd)
-    m = mark("v", V.tensor_tensor_scan(T.vi[:], T.ones[:], T.dlb[:], T.ps_d[:, 0:1], A.mult, A.subtract))
-    after("v", m)
-    m = mark("v", V.tensor_tensor(T.vm[:], T.vi[:], T.dlb[:], A.mult))
-    after("v", m)
-    m_vl = mark("v", V.tensor_scalar(T.vl[:], T.vm[:], -1.0, None, A.mult))
-    wait("v", "sval", 48)
-    after("v", m_bl)
-    m = mark("v", V.tensor_scalar(T.va[:], T.vali[:], T.sl[:, 0:1], T.bl[:, 0:1], A.mult, A.add))
-    after("v", m, m_vl)
-    m_data = mark("v", V.tensor_scalar(T.data[:], T.va[:, 0:776].indirect(T.vl[:, 0:C]), 255, None, A.bitwise_and))
+    after("v", m_dm, m_pd)
+    m_vl = mark("v", V.tensor_scalar(T.vl[:], T.dm[:], T.ps_d[:, 0:1], 0.0, A.add, A.max))
+    for k, mk in ((0, m_c0), (1, m_c1), (2, m_c2)):
+        after("y", m_vb, mk)
+        g.sync.dma_start(T.vb[k::16, 8:776], T["c%d" % k][:]).then_inc(S.slan, 16)
+    after("s", m_vl, m_vb0)
+    wait("s", "slan", 48)
+    m_data = mark("s", g.scalar.activation(T.data[:], T.vb[:, 0:776].indirect(T.vl[:, 0:C]), ACT.Copy))
 
-    m_iota = mark("g", g.iota(T.pi[:], [[0, 1]], 0, 1))
-    m_i1 = mark("g", g.iota(T.i1[:], [[1, C]], 1, 0, allow_small_or_imprecise_dtypes=True))
-    after("g", m_four)
-    m = mark("g", g.affine_select(T.sh0[:], T.four[:], [[1, 128]], A.is_equal, 0.0, -1, -1))
-    after("g", m)
-    m_sh = mark("g", g.affine_select(T.sh[:], T.sh0[:], [[0, 8], [1, 16]], A.is_gt, 0.0, 0, 0))
+    after("g", m_zz)
+    m_sh0 = mark("g", g.affine_select(T.sh[:], T.zz[:], [[1, 144]], A.not_equal, 4.0, -1, -1))
     m_bd = mark("g", g.affine_select(T.bd[:], T.t1[:], [[16, 8], [0, 16]], A.is_ge, 0.0, 15, -1))
-    m_wr = mark("g", g.affine_select(T.wr[:], T.four[:], [[-16, 8], [-1000, 16]], A.is_equal, 0.0, -15, 1))
-    after("g", m_zb8)
-    m = mark("g", g.affine_select(T.w8a[:], T.zb8[:], [[-16, 8]], A.not_equal, 1.0, 0, 1))
-    after("g", m)
-    m = mark("g", g.affine_select(T.w8b[:], T.w8a[:], [[-16, 8]], A.not_equal, 256.0, -1, 1))
-    after("g", m)
-    m_w8 = mark("g", g.affine_select(T.w8c[:], T.w8b[:], [[-16, 8]], A.not_equal, 65536.0, -2, 1))
+
+    m_rlk = mark("v", V.tensor_scalar(T.rlk[:], T.rli[:], 128.0, None, A.mult))
+    m_ll = mark("v", V.tensor_scalar(T.ll[:], T.sc[:, 0:C], -2.5, None, A.add))
+    if q:
+        m_wz = mark("v", V.memset(T.wr[:], 0.0))
+    after("v", m_rlk)
+    m_bb = mark("v", V.tensor_tensor(T.bb[:], T.sc[:, 0:C], T.rlk[:], A.add))
+    m_onesf = mark("v", V.memset(T.onesf[:], 1.0))
+    m_fv = mark("v", V.memset(T.win[:, w2:w2 + 1024], -0.125))
+    after("v", m_sh0)
+    if q:
+        after("v", m_wz)
+        m_wr = mark("v", V.tensor_copy(T.wr[:, 0:128:16], T.sh[:, 16:144:16]))
+        after("v", m_wr)
+    m_sh = mark("v", V.memset(T.sh[:, 0:144:16], 0.0))
+    m_fv = mark("v", V.memset(T.win[:, w2 + 1024:w2 + 2048], -0.125))
+    m_fv = mark("v", V.memset(T.win[:, w2 + 2048:w1], -0.125))
     after("g", m_onesf)
     m_id = mark("g", g.affine_select(T.ident[:], T.onesf[:], [[-1, 128]], A.is_equal, 0.0, 0, 1))
 
-    m_st = mark("v", V.tensor_scalar(T.st[:], T.rlb[:], -1.0, 1.0, A.mult, A.add))
-    m_rl4 = mark("v", V.tensor_scalar(T.rl4[:], T.rlb[:], 4.0, None, A.mult))
-    after("v", m_iota, m_i1)
-    m_nn = mark("v", V.tensor_tensor(T.nn[:], T.i1[:], T.sc[:, 0:C], A.subtract))
-    m_pa = mark("v", V.tensor_scalar(T.pa[:], T.pi[:], 15, None, A.bitwise_and))
-    after("v", m_nn)
-    m_ns = mark("v", V.tensor_tensor(T.ns[:], T.nn[:], T.st[:], A.mult))
-    after("v", m_pa)
-    k0 = 1.0 * C * 16 * q
-    m_kl = mark("v", V.tensor_scalar(T.kl[:], T.pa[:], 1.0 * C, k0 - 2.5, A.mult, A.add))
-    m_kz = mark("v", V.tensor_scalar(T.kz[:], T.pa[:], 1.0 * C, k0 - 1.0 - 512.0 * b0, A.mult, A.add))
-    after("v", m_ns)
-    m_d1 = mark("v", V.tensor_tensor(T.d1[:], T.ns[:], T.rl4[:], A.add))
-    after("v", m_kl)
-    m_ll = mark("v", V.tensor_scalar(T.ll[:], T.nn[:], T.kl[:, 0:1], None, A.add))
-    m_fv = mark("v", V.memset(T.win[:, 5632:W], 0.0))
-
-    after("p", m_sh, m_it)
-    m_pc = mark("p", g.tensor.matmul(T.ps_c[:, 0:1], T.sh[:], T.sc[:, 2 * C - 1:2 * C], True, q == 0))
+    after("p", m_it, m_sh)
     m_pb = mark("p", g.tensor.matmul(T.ps_b[:, 0:1], T.lt[:], T.sc[:, C - 1:C], True, q == 0))
+    m_pc = mark("p", g.tensor.matmul(T.ps_c[:, 0:1], T.sh[:, 0:128], T.sc[:, C + 7:C + 8], True, q == 0))
     if q:
         after("p", m_wr, m_bd)
         tot = sum(len(first_engines(topo, cores, j)[q]) for j in range(q))
         wait("p", "rcnt", tot)
-        m_pc = mark("p", g.tensor.matmul(T.ps_c[:, 0:1], T.wr[:], T["cm%d" % (q - 1)][:, C:C + 1], False, True))
         for j in range(q):
             m_pb = mark("p", g.tensor.matmul(T.ps_b[:, 0:1], T.bd[:], T["cm%d" % j][:, 0:1], False, j == q - 1))
-    after("v", m_pc, m_d1)
-    m_zl = mark("v", V.tensor_tensor_scan(T.zl[:], T.rlb[:], T.d1[:], T.ps_c[:, 0:1], A.mult, A.add))
+        m_pc = mark("p", g.tensor.matmul(T.ps_c[:, 0:1], T.wr[:], T["cm%d" % (q - 1)][:, 8:9], False, True))
     after("v", m_pb, m_ll)
-    m = mark("v", V.tensor_scalar(T.si[:], T.ll[:], T.ps_b[:, 0:1], 0.25, A.add, A.mult))
-    after("v", m)
-    m = mark("v", V.tensor_scalar(T.tt[:], T.si[:], 28.0, T.ps_b[:, 0:1], A.mult, A.add))
-    after("v", m, m_zl)
-    m = mark("v", V.tensor_tensor(T.oo[:], T.tt[:], T.zl[:], A.add))
-    after("v", m, m_kz)
-    m_ol = mark("v", V.tensor_scalar(T.ol[:], T.oo[:], T.kz[:, 0:1], None, A.add))
+    m_si = mark("v", V.tensor_scalar(T.si[:], T.ll[:], T.ps_b[:, 0:1], 0.25, A.add, A.mult))
+    after("v", m_pc, m_bb)
+    m_zl = mark("v", V.tensor_tensor_scan(T.zl[:], T.four[:], T.bb[:], T.ps_c[:, 0:1], A.add, A.min))
+    after("v", m_si)
+    m_tt = mark("v", V.tensor_scalar(T.tt[:], T.si[:], 28.0, T.ps_b[:, 0:1], A.mult, A.add))
+    after("v", m_tt, m_zl)
+    m_ol = mark("v", V.tensor_tensor(T.ol[:], T.tt[:], T.zl[:], A.add))
     after("v", m_ol, m_data, m_fv, m_fs)
     m_sct = mark("v", V.tensor_copy(T.win[:, 0:W].indirect(T.ol[:, 0:C]), T.data[:]))
 
     others = [(q + 1) % N, (q + 3) % N, (q + 2) % N]
-    dests = [d for d in others if topo.chip(cores[d]) != topo.chip(core)]
-    dests += [d for d in others if d not in dests]
-    after("p", m_sct, m_w8, m_po)
+    off = off_chip(topo, cores, q)
+    dests = [d for d in others if d in off] + [d for d in others if d not in off]
+    after("p", m_sct, m_bd, m_po)
     mp = {}
     for d in dests + [q]:
-        for b in range(BL):
-            ins = g.tensor.matmul(T["ps_o%d" % d][:, b0 + b:128:16], T.win[:, 512 * b + d:512 * b + 512:4], T.w8c[:], True, True)
+        for b in range(b0, b0 + BL):
+            c = 512 * b + d + 1
+            ins = g.tensor.matmul(T["ps_o%d" % d][:, b:128:16], T.win[:, c:c + 509:4], T.bd[:, 0:128:16], True, True)
         mp[d] = mark("p", ins)
     mo = {}
     for d in dests + [q]:
-        after("s", mp[d])
-        mo[d] = mark("s", g.scalar.activation(T["ob%d" % d][:], T["ps_o%d" % d][:, 0:128], ACT.Copy))
+        after("v", mp[d])
+        mo[d] = mark("v", V.tensor_copy(T["ob%d" % d][:], T["ps_o%d" % d][:, 0:128]))
         if d != q:
             after("g", mo[d])
             a = topo.addr(cores[d])
+            e = data_engines(topo, cores, q, d)
             g.remote_dma(out_ap=T["rc%d" % q][:], in_ap=T["ob%d" % d][:], remote_sem=S["rd%d" % q], local_sem=S.lr,
-                         pid=a[1], routing_id=a[0], dma_engine_mask=topo.mask(core, cores[d]))
-            lr += len(topo.engines(core, cores[d]))
+                         pid=a[1], routing_id=a[0], dma_engine_mask=bits(e))
+            lr += len(e)
 
     after("p", mo[q], m_id)
     mark("p", g.tensor.matmul(T.ps_y[:, 0:128], T["ob%d" % q][:], T.ident[:], True, False))
     src = [(q + 3) % N, (q + 2) % N, (q + 1) % N]
+    src = [j for j in src if j == 0] + [j for j in src if j != 0]
     for i, j in enumerate(src):
-        wait("p", "rd%d" % j, len(topo.engines(cores[j], core)))
+        wait("p", "rd%d" % j, len(data_engines(topo, cores, j, q)))
         m_y = mark("p", g.tensor.matmul(T.ps_y[:, 0:128], T["rc%d" % j][:], T.ident[:], False, i == len(src) - 1))
     after("v", m_y)
-    m_ys = mark("v", V.tensor_scalar(T.ysb[:], T.ps_y[:, 0:128], -2.0, None, A.add))
+    m_ys = mark("v", V.tensor_scalar(T.ysb[:], T.ps_y[:, 0:128], 6.0, None, A.add))
     after("y", m_ys)
     g.sync.dma_start(T.y[:], T.ysb[:]).then_inc(S.sy, 16)
     g.sync.wait_ge(S.sy, 16)

from concourse.bass import DstId, RemoteDMATransfer
from concourse.mybir import dt, AluOpType, AxisListType, ActivationFunctionType

N = 4
C = 48
BL = 12
W = 8208
SCRATCH = {
    "rli": ("sbuf", [128, C], "int32"),
    "dli": ("sbuf", [128, C], "int32"),
    "vali": ("sbuf", [128, C], "int32"),
    "rlb": ("sbuf", [128, C], "bfloat16"),
    "dlb": ("sbuf", [128, C], "bfloat16"),
    "sc": ("sbuf", [128, 64], "bfloat16"),
    "dsc": ("sbuf", [128, C], "bfloat16"),
    "nulk": ("sbuf", [128, C], "float32"),
    "dm": ("sbuf", [128, C], "float32"),
    "vl": ("sbuf", [128, C], "uint16"),
    "c0": ("sbuf", [128, C], "bfloat16"),
    "c1": ("sbuf", [128, C], "bfloat16"),
    "c2": ("sbuf", [128, C], "bfloat16"),
    "rr": ("sbuf", [128, C], "float32"),
    "rlk": ("sbuf", [128, C], "bfloat16"),
    "bb": ("sbuf", [128, C], "bfloat16"),
    "ll": ("sbuf", [128, C], "float32"),
    "zl": ("sbuf", [128, C], "float32"),
    "si": ("sbuf", [128, C], "int32"),
    "tt": ("sbuf", [128, C], "float32"),
    "ol": ("sbuf", [128, C], "uint16"),
    "vb": ("sbuf", [128, 776], "bfloat16"),
    "data": ("sbuf", [128, 768], "bfloat16"),
    "win": ("sbuf", [128, W], "bfloat16"),
    "ones": ("sbuf", [128, 128], "bfloat16"),
    "four": ("sbuf", [128, C], "bfloat16"),
    "zz": ("sbuf", [128, 144], "bfloat16"),
    "onesf": ("sbuf", [128, 128], "float32"),
    "t1": ("sbuf", [128, 128], "bfloat16"),
    "bd": ("sbuf", [128, 128], "bfloat16"),
    "lt": ("sbuf", [128, 128], "bfloat16"),
    "sh": ("sbuf", [128, 144], "bfloat16"),
    "wr": ("sbuf", [128, 128], "bfloat16"),
    "ident": ("sbuf", [128, 128], "float32"),
    "ysb": ("sbuf", [128, 128], "float32"),
    "ps_d": ("psum", [128, 512], "float32"),
    "ps_b": ("psum", [128, 512], "float32"),
    "ps_c": ("psum", [128, 512], "float32"),
    "ps_y": ("psum", [128, 512], "float32"),
}
for _q in range(N):
    SCRATCH["cm%d" % _q] = ("sbuf", [128, 16], "bfloat16")
    SCRATCH["rc%d" % _q] = ("sbuf", [128, 128], "float32")
    SCRATCH["ob%d" % _q] = ("sbuf", [128, 128], "float32")
    SCRATCH["ps_o%d" % _q] = ("psum", [128, 512], "float32")
SEMAPHORES = ["srl", "sdl", "sval", "slan", "sy", "sv", "sg", "ss", "sp", "rcnt", "lr"] + ["rd%d" % q for q in range(N)]


def off_chip(topo, cores, q):
    return [d for d in range(N) if topo.chip(cores[d]) != topo.chip(cores[q])]


def first_engines(topo, cores, q):
    res = {}
    used = []
    for i, d in enumerate(x for x in off_chip(topo, cores, q) if x > q):
        e = topo.engines(cores[q], cores[d])
        n = len(e) // 2
        res[d] = e[i * n:(i + 1) * n]
        used += e
    for d in range(q + 1, N):
        if d not in res:
            e = [x for x in topo.engines(cores[q], cores[d]) if x not in used]
            res[d] = e[:4]
    return res


def data_engines(topo, cores, q, d):
    e = topo.engines(cores[q], cores[d])
    off = off_chip(topo, cores, q)
    if d not in off:
        e = [x for x in e if x not in topo.engines(cores[q], cores[off[0]])]
    return e


def bits(e):
    return sum(1 << x for x in e)


def rank_program(g, core, T, topo):
    rank = T.rank_of(core)
    if rank is None:
        return
    cores = list(T.cores)
    q = rank
    S = T.sem
    A = AluOpType
    ACT = ActivationFunctionType
    queues = {"v": g.vector, "s": g.scalar, "p": g.tensor, "g": g, "y": g.sync}
    own = {"v": "sv", "s": "ss", "p": "sp", "g": "sg"}
    done = {"v": 0, "s": 0, "p": 0, "g": 0}
    seen = {}

    def wait(qn, sem, val):
        if val > seen.get((qn, sem), 0):
            seen[(qn, sem)] = val
            queues[qn].wait_ge(S[sem], val)

    def after(qn, *marks):
        for (o, c) in marks:
            wait(qn, own[o], c)

    def mark(qn, ins):
        ins.then_inc(S[own[qn]], 1)
        done[qn] += 1
        return (qn, done[qn])

    V = g.vector
    b0 = 24 * q // 16
    w0 = 512 * b0
    w1 = w0 + 512 * BL + 16
    g.sync.dma_start(T.rli[:], T.rl[:]).then_inc(S.srl, 16)
    g.scalar.dma_start(T.dli[:], T.dl[:]).then_inc(S.sdl, 16)
    g.sync.dma_start(T.vali[:], T.val[:]).then_inc(S.sval, 16)
    m_ones = mark("v", V.memset(T.ones[:], 1.0))
    m_f0 = mark("v", V.memset(T.win[:, w0:w0 + 512], -0.125))
    m_four = mark("v", V.memset(T.four[:], 4.0))
    m_zz = mark("v", V.memset(T.zz[:], 0.0))
    m_vb0 = mark("v", V.memset(T.vb[:, 0:8], -0.0625))
    m_vb = mark("v", V.memset(T.vb[:, 8:776], 0.0))

    after("g", m_ones)
    m_t1 = mark("g", g.affine_select(T.t1[:], T.ones[:], [[-16, 8], [0, 16]], A.is_ge, 0.0, 0, 1))
    after("g", m_t1)
    m_lt = mark("g", g.affine_select(T.lt[:], T.t1[:], [[1, 128]], A.is_gt, 0.0, 0, -1))

    after("p", m_f0)
    for d in range(N):
        m_po = mark("p", g.tensor.matmul(T["ps_o%d" % d][:, 0:128], T.ones[0:16, 0:128], T.win[0:16, w0:w0 + 128], True, True))

    after("s", m_f0)
    m = mark("s", g.scalar.activation(T.win[:, w0 + 512:w0 + 1024], T.win[:, w0:w0 + 512], ACT.Copy))
    after("s", m)
    for k in range(1, 3):
        m_fs = mark("s", g.scalar.activation(T.win[:, w0 + 1024 * k:w0 + 1024 * k + 1024], T.win[:, w0:w0 + 1024], ACT.Copy))
    w2 = w0 + 3072

    wait("v", "srl", 16)
    m_rlb = mark("v", V.tensor_copy(T.rlb[:], T.rli[:]))
    after("v", m_rlb)
    m_nn = mark("v", V.tensor_tensor_scan(T.sc[:, 0:C], T.ones[:, 0:C], T.rlb[:], 0.0, A.add, A.subtract))
    m_it = mark("v", V.tensor_tensor_scan(T.sc[:, C:C + 8], T.rlb[:, C - 8:C], T.rlb[:, C - 8:C], 0.0, A.mult, A.add))
    fe = first_engines(topo, cores, q)
    lr = 0
    if fe:
        after("g", m_it)
        tr = []
        for d in sorted(fe):
            a = topo.addr(cores[d])
            tr.append(RemoteDMATransfer(dst_ids=[DstId(rid=a[0], pnc=a[1])], dma_engine_mask=bits(fe[d]),
                                        remote_sem=S.rcnt, src=T.sc[:, C - 1:C + 8], dst=T["cm%d" % q][:, 0:9]))
            lr += len(fe[d])
        g.remote_dma_fused(tr, local_sem=S.lr)

    wait("v", "sdl", 16)
    m_dlb = mark("v", V.tensor_copy(T.dlb[:], T.dli[:]))
    wait("v", "sval", 16)
    m_c0 = mark("v", V.tensor_copy(T.c0[:], T.vali[:]))
    after("v", m_dlb)
    m_ds = mark("v", V.tensor_tensor_scan(T.dsc[:], T.ones[:, 0:C], T.dlb[:], 0.0, A.mult, A.add))
    after("v", m_c0)
    m_rr = mark("v", V.tensor_tensor(T.rr[:], T.vali[:], T.c0[:], A.subtract))
    m_nk = mark("v", V.tensor_scalar(T.nulk[:], T.dlb[:], 4096.0, -4089.0, A.mult, A.add))
    after("v", m_rr)
    m_c1 = mark("v", V.tensor_copy(T.c1[:], T.rr[:]))
    after("v", m_nk)
    m_dm = mark("v", V.tensor_tensor(T.dm[:], T.dsc[:], T.nulk[:], A.add))
    after("v", m_c1)
    m_c2 = mark("v", V.tensor_tensor(T.c2[:], T.rr[:], T.c1[:], A.subtract))
    after("p", m_ds, m_lt)
    m_pd = mark("p", g.tensor.matmul(T.ps_d[:, 0:1], T.lt[:], T.dsc[:, C - 1:C], True, True))
    after("v", m_dm, m_pd)
    m_vl = mark("v", V.tensor_scalar(T.vl[:], T.dm[:], T.ps_d[:, 0:1], 0.0, A.add, A.max))
    for k, mk in ((0, m_c0), (1, m_c1), (2, m_c2)):
        after("y", m_vb, mk)
        g.sync.dma_start(T.vb[k::16, 8:776], T["c%d" % k][:]).then_inc(S.slan, 16)
    after("s", m_vl, m_vb0)
    wait("s", "slan", 48)
    m_data = mark("s", g.scalar.activation(T.data[:], T.vb[:, 0:776].indirect(T.vl[:, 0:C]), ACT.Copy))

    after("g", m_zz)
    m_sh0 = mark("g", g.affine_select(T.sh[:], T.zz[:], [[1, 144]], A.not_equal, 4.0, -1, -1))
    m_bd = mark("g", g.affine_select(T.bd[:], T.t1[:], [[16, 8], [0, 16]], A.is_ge, 0.0, 15, -1))

    m_rlk = mark("v", V.tensor_scalar(T.rlk[:], T.rli[:], 128.0, None, A.mult))
    m_ll = mark("v", V.tensor_scalar(T.ll[:], T.sc[:, 0:C], -2.5, None, A.add))
    if q:
        m_wz = mark("v", V.memset(T.wr[:], 0.0))
    after("v", m_rlk)
    m_bb = mark("v", V.tensor_tensor(T.bb[:], T.sc[:, 0:C], T.rlk[:], A.add))
    m_onesf = mark("v", V.memset(T.onesf[:], 1.0))
    m_fv = mark("v", V.memset(T.win[:, w2:w2 + 1024], -0.125))
    after("v", m_sh0)
    if q:
        after("v", m_wz)
        m_wr = mark("v", V.tensor_copy(T.wr[:, 0:128:16], T.sh[:, 16:144:16]))
        after("v", m_wr)
    m_sh = mark("v", V.memset(T.sh[:, 0:144:16], 0.0))
    m_fv = mark("v", V.memset(T.win[:, w2 + 1024:w2 + 2048], -0.125))
    m_fv = mark("v", V.memset(T.win[:, w2 + 2048:w1], -0.125))
    after("g", m_onesf)
    m_id = mark("g", g.affine_select(T.ident[:], T.onesf[:], [[-1, 128]], A.is_equal, 0.0, 0, 1))

    after("p", m_it, m_sh)
    m_pb = mark("p", g.tensor.matmul(T.ps_b[:, 0:1], T.lt[:], T.sc[:, C - 1:C], True, q == 0))
    m_pc = mark("p", g.tensor.matmul(T.ps_c[:, 0:1], T.sh[:, 0:128], T.sc[:, C + 7:C + 8], True, q == 0))
    if q:
        after("p", m_wr, m_bd)
        tot = sum(len(first_engines(topo, cores, j)[q]) for j in range(q))
        wait("p", "rcnt", tot)
        for j in range(q):
            m_pb = mark("p", g.tensor.matmul(T.ps_b[:, 0:1], T.bd[:], T["cm%d" % j][:, 0:1], False, j == q - 1))
        m_pc = mark("p", g.tensor.matmul(T.ps_c[:, 0:1], T.wr[:], T["cm%d" % (q - 1)][:, 8:9], False, True))
    after("v", m_pb, m_ll)
    m_si = mark("v", V.tensor_scalar(T.si[:], T.ll[:], T.ps_b[:, 0:1], 0.25, A.add, A.mult))
    after("v", m_pc, m_bb)
    m_zl = mark("v", V.tensor_tensor_scan(T.zl[:], T.four[:], T.bb[:], T.ps_c[:, 0:1], A.add, A.min))
    after("v", m_si)
    m_tt = mark("v", V.tensor_scalar(T.tt[:], T.si[:], 28.0, T.ps_b[:, 0:1], A.mult, A.add))
    after("v", m_tt, m_zl)
    m_ol = mark("v", V.tensor_tensor(T.ol[:], T.tt[:], T.zl[:], A.add))
    after("v", m_ol, m_data, m_fv, m_fs)
    m_sct = mark("v", V.tensor_copy(T.win[:, 0:W].indirect(T.ol[:, 0:C]), T.data[:]))

    others = [(q + 1) % N, (q + 3) % N, (q + 2) % N]
    off = off_chip(topo, cores, q)
    dests = [d for d in others if d in off] + [d for d in others if d not in off]
    after("p", m_sct, m_bd, m_po)
    mp = {}
    for d in dests + [q]:
        for b in range(b0, b0 + BL):
            c = 512 * b + d + 1
            ins = g.tensor.matmul(T["ps_o%d" % d][:, b:128:16], T.win[:, c:c + 509:4], T.bd[:, 0:128:16], True, True)
        mp[d] = mark("p", ins)
    mo = {}
    for d in dests + [q]:
        after("v", mp[d])
        mo[d] = mark("v", V.tensor_copy(T["ob%d" % d][:], T["ps_o%d" % d][:, 0:128]))
        if d != q:
            after("g", mo[d])
            a = topo.addr(cores[d])
            e = data_engines(topo, cores, q, d)
            g.remote_dma(out_ap=T["rc%d" % q][:], in_ap=T["ob%d" % d][:], remote_sem=S["rd%d" % q], local_sem=S.lr,
                         pid=a[1], routing_id=a[0], dma_engine_mask=bits(e))
            lr += len(e)

    after("p", mo[q], m_id)
    mark("p", g.tensor.matmul(T.ps_y[:, 0:128], T["ob%d" % q][:], T.ident[:], True, False))
    src = [(q + 3) % N, (q + 2) % N, (q + 1) % N]
    src = [j for j in src if j == 0] + [j for j in src if j != 0]
    for i, j in enumerate(src):
        wait("p", "rd%d" % j, len(data_engines(topo, cores, j, q)))
        m_y = mark("p", g.tensor.matmul(T.ps_y[:, 0:128], T["rc%d" % j][:], T.ident[:], False, i == len(src) - 1))
    after("v", m_y)
    m_ys = mark("v", V.tensor_scalar(T.ysb[:], T.ps_y[:, 0:128], 6.0, None, A.add))
    after("y", m_ys)
    g.sync.dma_start(T.y[:], T.ysb[:]).then_inc(S.sy, 16)
    g.sync.wait_ge(S.sy, 16)
    for qn in ("v", "s", "p", "g"):
        if done[qn]:
            wait("g", own[qn], done[qn])
    wait("g", "lr", lr)
